import numpy as np, ml_dtypes
CORES = [3,11,19,27,35,43,51,59]
N = 8
BF = ml_dtypes.bfloat16
def gentries(a):
    return np.ascontiguousarray(a.reshape(8, 16, -1).transpose(0, 2, 1)).reshape(8, -1)
def gtable(e):
    e = np.asarray(e); return np.ascontiguousarray(e.reshape(8, -1, 16).transpose(0, 2, 1)).reshape(128, -1).astype(np.int32)
B, H, D, O, CAP, RO = 2048, 4096, 2048, 2048, 192, 3
K2, K3, K5 = 37, 611, 1237
def parts(rng):
    wt = (rng.choice(np.array([12, 20, 40, 64]), (N, 8, 16, 1)) * rng.random((N, 8, 16, B))).astype(np.int64)
    kid = rng.integers(0, B // 16, (N, 8, 16, B)); noise = rng.integers(0, 64, (N, 8, 16, H))
    for q in range(N):
        for g in rng.permutation(8)[:2]: kid[q, g] = rng.integers(0, B // 16, 8)[rng.integers(0, 8, (16, B))]
    room = np.minimum(rng.integers(60, 256, (N, 8, 1, D)) + rng.integers(0, 41, (N, 8, 16, D)), 255)
    room = np.where(rng.random(room.shape) < 0.01, rng.integers(0, 60, room.shape), room)
    need = (rng.integers(10, 201, (N, 8, 1, O)) * rng.random((N, 8, 16, O))).astype(np.int64)
    return wt, kid, noise, room, need, rng.integers(0, B, (N, 8, O)), rng.integers(0, H, (N, 8, O))
def sure(rng, wt, noise, q, g, win):
    noise[q, g] = rng.integers(8, 64, (16, H)); v = rng.integers(0, 8, (16, B)); v[win, np.arange(B)] = 63; wt[q, g] = v
def pack(wt, kid, noise, room, need, begin, salt):
    a = [np.ascontiguousarray(v.reshape(N, 128, -1)).astype(np.float32).astype(BF) for v in (wt, kid, noise, room, need)]
    return {"wt": a[0], "kid": a[1], "noise": a[2], "room": a[3], "need": a[4], "begin": np.stack([gtable(v) for v in begin]), "salt": np.stack([gtable(v) for v in salt])}
def setup_inputs(rng):
    return pack(*parts(rng))
def setup_inputs_cap(rng):
    wt, kid, noise, room, need, begin, salt = parts(rng)
    win = rng.integers(0, 16, (N, 8, B)); win[..., :16] = np.arange(16)
    win[:, 6] = (np.arange(B) & (N - 1)) + N * rng.integers(0, 16 // N, (N, B)); room[:, 6] = np.maximum(room[:, 6], 200)
    noise = rng.integers(8, 64, noise.shape); wt = rng.integers(0, 8, wt.shape); np.put_along_axis(wt, win[:, :, None, :], 63, 2)
    for q in range(N):
        for g in range(8):
            r = (q + 1 + int(rng.integers(0, N - 1))) % N; n = (CAP, CAP + 1, CAP - 1, 0, O, 1, CAP, CAP)[g]
            others = np.array([i for i in range(N) if i != r])
            to = rng.permutation(np.concatenate([np.full(n, r), rng.choice(others, O - n)]))
            if g < 2:
                i = np.flatnonzero(to == r)[-1]; to[i] = to[O - 1]; to[O - 1] = r
            if g == 6: to = rng.permutation(np.arange(O) & (N - 1))
            if g == 7:
                to = rng.choice(others, O); to[np.argsort(rng.permutation(16)[np.arange(O) % 16], kind="stable")[:n]] = r
            for i in range(N):
                m = np.flatnonzero(to == i); begin[q, g, m] = rng.choice(np.flatnonzero((win[q, g] & (N - 1)) == i), len(m))
    return pack(wt, kid, noise, room, need, begin, salt)
def setup_inputs_ties(rng):
    wt, kid, noise, room, need, begin, salt = parts(rng)
    wt = rng.integers(0, 3, wt.shape) * (rng.random((N, 8, 1, B)) > 0.1); noise = rng.integers(0, 3, noise.shape)
    wt = np.where(rng.random((N, 8, 1, B)) < 0.15, rng.integers(1, 3, (N, 8, 1, B)), wt)
    noise = np.where(rng.random((N, 8, 1, H)) < 0.15, rng.integers(1, 3, (N, 8, 1, H)), noise) * (rng.random((N, 8, 1, H)) > 0.05)
    room = np.where(rng.random(room.shape) < 0.003, 0, np.zeros(room.shape, np.int64) + rng.choice(np.array([99, 100, 100, 101, 255]), (N, 8, 1, D)))
    need = np.where(rng.random(need.shape) < 0.1, rng.choice(np.array([0, 99, 100, 101, 255]), (N, 8, 1, O)), 0)
    begin[:, 1::4] = rng.choice(np.array([0, B - 1]), (N, 2, O)); salt[:, 2::4] = rng.choice(np.array([0, H - 1]), (N, 2, O))
    kid[:, 7] = rng.integers(0, B // 16, (N, 16, B)); win = rng.integers(0, 16, (N, B))
    for q in range(N): sure(rng, wt, noise, q, 7, win[q])
    to = 16 * np.take_along_axis(kid[:, 7], win[:, None, :], 1)[:, 0] + win
    few = rng.integers(0, B, (N, 24)); begin[:, 7] = np.take_along_axis(few, rng.integers(0, 24, (N, O)), 1)
    need[:, 7] = np.maximum(need[:, 7], 1); room[:, 7] = 0
    for s in range(2 * (RO - 1), -1, -2):
        b = np.take_along_axis(to, (few + K5 * s) & (B - 1), 1); own = b & (N - 1)
        room[own, 7, :, to[own, b] & (D - 1)] = 255 if s == 2 * (RO - 1) else 0
    return pack(wt, kid, noise, room, need, begin, salt)
def setup_inputs_again(rng):
    wt, kid, noise, room, need, begin, salt = parts(rng)
    for q in range(N):
        for g in range(8): kid[q, g] = rng.integers(0, B // 16, 2)[rng.integers(0, 2, (16, B))]
        kid[q, 3] = rng.integers(0, B // 16); wt[q, 3] = 0; wt[q, 3, rng.integers(0, 16)] = 63
    noise[:, 3] = np.maximum(noise[:, 3], 1); room = np.maximum(room, 200)
    begin[:, ::2] = rng.choice(np.array([0, 5, B // 2, B - 1]), (N, 4, O)); salt[:, ::2] = rng.choice(np.array([0, 1, H // 2, H - 1]), (N, 4, O))
    r = int(rng.integers(0, N)); c = r + N * int(rng.integers(0, 16 // N))
    win = (np.arange(B) & (N - 1)) + N * rng.integers(0, 16 // N, (N, B)); win[r, r::N] = c; kid[r, 5, c, r::N] = kid[r, 5, c, r]
    for q in range(N): sure(rng, wt, noise, q, 5, win[q])
    begin[:, 5] = r + N * rng.integers(0, B // N, (N, O))
    return pack(wt, kid, noise, room, need, begin, salt)
def setup_inputs_full(rng):
    wt, kid, noise, room, need, begin, salt = parts(rng); q = rng.permutation(N)
    need = np.where(rng.random((N, 8, 1, O)) < 0.05, 255, np.maximum(need, 1)); room[q[0]] = 0; need[q[1]] = 0; room[q[2]] = 255
    r, a = int(q[2]), int(q[3]); walk = (K5 * np.arange(B)) & (B - 1)
    for g in range(8):
        win = rng.choice(np.array([c for c in range(16) if c & (N - 1) != r]), B); win[walk[::8]] = r + N * rng.integers(0, 16 // N, B // 8)
        sure(rng, wt, noise, a, g, win)
        at = rng.integers(1, 4, O); at[rng.permutation(O)[:CAP // 2]] = 0
        begin[a, g] = walk[8 * rng.integers(0, B // 8, O) + at]
    return pack(wt, kid, noise, room, need, begin, salt)
def setup_inputs_spread(rng):
    wt, kid, noise, room, need, begin, salt = parts(rng); ex = np.array([0.3, 1.0, 3.0])
    wt = np.minimum((64 * rng.random(wt.shape) ** rng.choice(ex, (N, 8, 1, B))).astype(np.int64), 63)
    noise = np.minimum((64 * rng.random(noise.shape) ** rng.choice(ex, (N, 8, 1, H))).astype(np.int64), 63)
    kid = np.minimum((B // 16 * rng.random(kid.shape) ** 3).astype(np.int64), B // 16 - 1)
    room = np.minimum((256 * rng.random(room.shape) ** rng.choice(np.array([0.0, 0.02, 0.1, 1.0]), (N, 8, 1, D))).astype(np.int64), 255)
    need = np.minimum((np.exp2(8 * rng.random((N, 8, 1, O))) * rng.random(need.shape)).astype(np.int64), 255)
    begin = np.minimum((B * rng.random((N, 8, O)) ** 2).astype(np.int64), B - 1); salt = np.minimum((H * rng.random((N, 8, O)) ** 3).astype(np.int64), H - 1)
    return pack(wt, kid, noise, room, need, begin, salt)
def check_inputs(d):
    bad = []
    for k, hi in (("wt", 63), ("kid", B // 16 - 1), ("noise", 63), ("room", 255), ("need", 255), ("begin", B - 1), ("salt", H - 1)):
        v = np.asarray(d[k]).astype(np.float32)
        if not np.all((v >= 0) & (v <= hi)): bad.append("range of " + k)
        if not np.all(v == np.floor(v)): bad.append("whole numbers in " + k)
    return bad
def columns(a):
    return np.ascontiguousarray(a.astype(np.float32).astype(np.int32).reshape(N, 8, 16, -1).transpose(0, 1, 3, 2))
def choose(w, k, z, r, b, h):
    g = np.arange(8)[None, :, None]
    c = np.argmax(w[r, g, b] * z[r, g, h], axis=-1)
    return 16 * k[r, g, b, c].astype(np.int64) + c
def reference(wt, kid, noise, room, need, begin, salt):
    w, k, z, rm, nd = columns(wt), columns(kid), columns(noise), columns(room), columns(need)
    be = np.stack([gentries(a) for a in begin]).astype(np.int64); sa = np.stack([gentries(a) for a in salt]).astype(np.int64)
    home = np.arange(N)[:, None, None]; g = np.arange(8)[None, :, None]
    t = np.zeros((N, 8, O), np.int64); one = np.full((N, 8, O), -1, np.int64); two = np.full((N, 8, O), -1, np.int64)
    for rnd in range(RO):
        takes = two < 0
        b0 = (be + K5 * t) & (B - 1)
        b1 = choose(w, k, z, home, b0, (sa + K2 * b0 + K3 * t) & (H - 1))
        own = b1 & (N - 1); goes = np.zeros((N, 8, O), bool)
        for r in range(N):
            m = (takes & (own == r)).astype(np.int64)
            goes = goes | ((m == 1) & (np.add.accumulate(m, axis=2) - m < CAP))
        d = choose(w, k, z, own, b1, (sa + K2 * b1 + K3 * t) & (H - 1)) & (D - 1)
        fits = np.all(nd <= rm[own, g, d], axis=-1)
        dev = own * D + d; keep = goes & fits & (dev != one)
        two = np.where(keep & (one >= 0), dev, two); one = np.where(keep & (one < 0), dev, one)
        t = t + np.where(goes, np.where(keep, 1, 2), 0)
    return {"ya": np.stack([gtable(a) for a in one]).astype(np.float32), "yb": np.stack([gtable(a) for a in two]).astype(np.float32)}

from concourse.bass import DstId, RemoteDMATransfer
from concourse.mybir import AluOpType, ActivationFunctionType

ALU = AluOpType
ACT = ActivationFunctionType
NR, CAP, RO = 8, 192, 3
KS = CAP // 16
NS = NR * CAP
NZ = 12
PDT = "float16"
F32, BF, I32, U16 = "float32", "bfloat16", "int32", "uint16"
BANKS = ("TA", "TB", "G0", "G1", "R0", "R1", "PL", "PF")
PARTS = ("pay", "ps", "st", "sts", "rmp", "R0x", "R1x", "R2x", "R3x")

SCRATCH = {"P": ("sbuf", [128, 2048], PDT), "ip": ("sbuf", [128, 128], PDT)}
for _dt, _bufs in (
        (BF, {"w": 2048, "kd": 2048, "nz": 4096, "rm": 2048, "rmp": 2048, "nd": 2048, "win": 6144, "pay": 1024, "st": 1024,
              "Z": 512 * NZ, "K": 512 * NZ, "cb": 144, "ch": 144, "co": 144, "cc": 144, "ik": 128, "iz": 128,
              "ob": 128, "obn": 128, "n1": 128, "n2": 128, "ccb": 128, "m": 1024, "sc": 1024, "cmp": NS,
              "R": NS + 16, "wb": NS, "Rg": 2048, "sf": 512, "fl": 384, "am": [16, 136]}),
        (F32, {"ones": 128, "i32": 128, "iperm": 128, "dk": 128, "dr": 512, "pf": 16, "row": 16, "grow": 128, "e16": 16,
               "g8": 8, "krow": 128, "dump": 128, "V": 640, "qs": 1024, "t": 128, "tb": 128, "go": 128, "base": 128,
               "cv": 128, "ne": 128, "one": 128, "two": 128, "none": 128, "D": 128, "B": 128, "AB": 256, "e": 128,
               "tf": 1024, "sb0": [35, 4], "sb1": [35, 4], "so": [128, 8], "ws": 6144, "ps": 1024, "sts": 1024, "c32": 2}),
        (I32, {"bg": 128, "sa": 128, "pi": 4, "xb": 640, "xh": 640, "si": 128, "ccl": 128, "ti": 256, "rhi": 96,
               "oi": 96, "ox": 96, "ok": 96, "oc": 96}),
        (U16, {"ob0": 640, "oh0": 640, "pos": 128, "pos2": 128, "oo": 96, "rb2": 96, "rh2": 96, "oxu": 96})):
    for _n, _s in _bufs.items():
        SCRATCH[_n] = ("sbuf", [128] + (_s if isinstance(_s, list) else [_s]), _dt)
for _n in BANKS:
    SCRATCH[_n] = ("psum", [128, 512], F32)
for _r in range(RO):
    for _s in "sl":
        SCRATCH["%sq%d" % (_s, _r)] = ("sbuf", [128, NR * 2 * KS], I32)
        SCRATCH["%sn%d" % (_s, _r)] = ("sbuf", [128, NS], BF)
        SCRATCH["%sr%d" % (_s, _r)] = ("sbuf", [128, NR * 2 * KS], BF)

LOADS = ["sa", "bg", "w", "nz", "kd", "rm", "nd"]
SEMAPHORES = (["cV", "cS", "cP", "cG", "loc", "oa", "obs"] + ["l" + n for n in LOADS]
              + ["a%s%d" % (k, r) for k in "qnr" for r in range(RO)])
AHEAD = 4


def rank_program(g, core, T, topo):
    me = T.rank_of(core)
    if me is None:
        return
    Q = {"V": g.vector, "S": g.scalar, "P": g.tensor, "G": g, "Y": g.sync}
    cnt = {"V": 0, "S": 0, "P": 0, "G": 0}
    known = {e: {} for e in Q}
    wr, rd = {}, {}

    def need(e, tok):
        if known[e].get(tok[1], 0) < tok[2]:
            Q[e].wait_ge(T.sem[tok[1]], tok[2])
            known[e][tok[1]] = tok[2]

    def deps(e, r, w):
        for k in r:
            if k in wr:
                need(e, wr[k])
        for k in w:
            for n, tok in enumerate([wr.get(k)] + rd.get(k, [])):
                if tok and (tok[0] != e or not (e == "P" or k in BANKS or (k in PARTS and n == 0))):
                    need(e, tok)

    def op(e, fn, r=(), w=()):
        deps(e, r, w)
        fn().then_inc(T.sem["c" + e], 1)
        cnt[e] += 1
        tok = (e, "c" + e, cnt[e])
        for k in r:
            rd.setdefault(k, []).append(tok)
        for k in w:
            wr[k] = tok
            rd[k] = []

    V, S, PE = g.vector, g.scalar, g.tensor

    def ts(out, in0, s1, o0, s2=None, o1=None, r=(), w=()):
        if o1 is None:
            op("V", lambda: V.tensor_scalar(out, in0, s1, None, o0), r, w)
        else:
            op("V", lambda: V.tensor_scalar(out, in0, s1, s2, o0, o1), r, w)

    def tt(out, a, b, o, r=(), w=()):
        op("V", lambda: V.tensor_tensor(out, a, b, o), r, w)

    def cp(e, out, a, r=(), w=()):
        if e == "V":
            op("V", lambda: V.tensor_copy(out, a), r, w)
        else:
            op("S", lambda: S.activation(out, a, ACT.Copy), r, w)

    def act(out, a, f, j, r, w):
        op("S", lambda: S.activation(out, a, f, bias=T.c32[:, j:j + 1]), r + ["c32"], w)

    def ms(ap, c, w):
        op("V", lambda: V.memset(ap, c), (), w)

    def mm(out, l, rh, st, sp, r=(), w=()):
        op("P", lambda: PE.matmul(out, l, rh, st, sp), r, w)

    def run(out, d0, d1, o1, r, w):
        op("V", lambda: V.tensor_tensor_scan(out, d0, d1, 0.0, ALU.add, o1), r, w)

    def blk(buf, j, n=1):
        return buf[:, 128 * j:128 * (j + n)]

    AND, SHR = ALU.bitwise_and, ALU.logical_shift_right

    src = {"bg": T.begin, "sa": T.salt, "w": T.wt, "nz": T.noise, "kd": T.kid, "rm": T.room, "nd": T.need}
    for n in LOADS:
        g.sync.dma_start(T[n][:], src[n][:]).then_inc(T.sem["l" + n], 16)
        wr[n] = ("D", "l" + n, 16)

    FL = {"allow_small_or_imprecise_dtypes": True}
    ms(T.ones[:], 1.0, ["ones"])
    op("G", lambda: g.iota(T.pi[:, 0:1], [[1, 1]], 0, 1), (), ["pi0"])
    op("G", lambda: g.affine_select(T.iperm[:], T.ones[:], [[-1, 16], [-16, 8]], ALU.is_equal, 0.0, 0, 1), ["ones"], ["iperm"])
    op("G", lambda: g.iota(T.krow[:], [[1, 128]], 0, 0, **FL), (), ["krow"])
    op("G", lambda: g.affine_select(T.i32[:], T.ones[:], [[-1, 128]], ALU.is_equal, 0.0, 0, 1), ["ones"], ["i32"])
    op("G", lambda: g.iota(T.row[:], [[1, 16]], 0, 0, **FL), (), ["row"])
    op("G", lambda: g.iota(T.grow[:], [[1, 8], [0, 16]], 0, 0, **FL), (), ["grow"])
    op("G", lambda: g.iota(T.c32[:], [[-64, 2]], 32, 0, **FL), (), ["c32"])
    ms(T.dk[:], 128.0, ["dk"])
    ms(T.am[:], 0.0, ["am"])
    for sbn in ("sb0", "sb1"):
        ms(T[sbn][:], 0.0, [sbn])
    ts(T.pi[:, 1:2], T.pi[:, 0:1], 15, AND, r=["pi0"], w=["pi1"])
    ts(T.pi[:, 2:3], T.pi[:, 0:1], 4, SHR, r=["pi0"], w=["pi2"])
    ms(T.dk[:, 0:128:16], -16777216.0, ["dk"])
    cp("V", T.am[:, :, 7:135:16], T.iperm[:], ["iperm"], ["am"])
    cp("V", T.pf[:, 0:2], T.pi[:, 1:3], ["pi1", "pi2"], ["pf0"])

    def offsets(t0, t1):
        n, key, tr = t1 - t0, "off%d" % t0, range(t0, t1)
        for t in tr:
            ts(blk(T.xb, t), T.bg[:], 1237 * t, ALU.add, r=["bg"], w=["xb%d" % t])
        ts(blk(T.xb, t0, n), blk(T.xb, t0, n), 2047, AND, r=["xb%d" % t for t in tr], w=["xb" + key])
        for t in tr:
            ts(blk(T.xh, t), blk(T.xb, t), 37, ALU.mult, 611 * t, ALU.add, r=["xb" + key], w=["xh%d" % t])
        cp("V", blk(T.ob0, t0, n), blk(T.xb, t0, n), ["xb" + key], ["b" + key])
        for t in tr:
            tt(blk(T.xh, t), blk(T.xh, t), T.sa[:], ALU.add, ["xh%d" % t, "sa"], ["xh%d" % t])
        ts(blk(T.xh, t0, n), blk(T.xh, t0, n), 4095, AND, r=["xh%d" % t for t in tr], w=["xh" + key])
        cp("V", blk(T.oh0, t0, n), blk(T.xh, t0, n), ["xh" + key], ["h" + key])

    ti = [blk(T.ti, j) for j in range(2)]
    tf = [blk(T.tf, j) for j in range(8)]
    ts(ti[0], T.sa[:], 63, AND, r=["sa"], w=["ti0"])
    ts(ti[1], T.sa[:], 6, SHR, r=["sa"], w=["ti1"])
    cp("V", blk(T.sf, 2), T.krow[:], ["krow"], ["sf2"])
    ts(blk(T.sf, 3), T.ones[:], T.pf[:, 0:1], ALU.mult, r=["ones", "pf0"], w=["sf3"])
    ts(blk(T.sf, 0, 2), T.ti[:], 1.0, ALU.mult, r=["ti0", "ti1"], w=["sf0"])
    offsets(0, 1)
    ts(T.ip[:], T.i32[:], 2048.0, ALU.mult, r=["i32"], w=["ip"])
    ts(T.iz[:], T.i32[:], 65536.0, ALU.mult, r=["i32"], w=["iz"])
    cp("V", T.ik[:], T.i32[:], ["i32"], ["ik"])

    def spread(h, buf, fields):
        for i in range(16):
            bank = "G%d" % (i // 8)
            for n, (f, j, key) in enumerate(fields):
                mm(T[bank][:, 64 * (i % 8):64 * (i % 8) + 64], T.am[:, i, 7 - f:135 - f],
                   buf[:, 128 * j + 64 * h:128 * j + 64 * h + 64], n == 0, n == len(fields) - 1, ["am", key], [bank, bank + "d"])

    def rows(fn, dst, key):
        for i in range(16):
            bank = "G%d" % (i // 8)
            fn(dst[:, i:1024:16], T[bank][:, 64 * (i % 8):64 * (i % 8) + 64], i, [bank + "d"], [bank, key])

    stat = [(3, 0, "sf0"), (4, 1, "sf0"), (5, 2, "sf2"), (6, 3, "sf3")]
    spread(0, T.sf, stat)
    rows(lambda o, p, i, r, w: cp("S", o, p, r, w), T.st, "st")
    act(T.w[:], T.w[:], ACT.Identity, 1, ["w"], ["w"])
    spread(1, T.sf, stat)
    rows(lambda o, p, i, r, w: act(o, p, ACT.Identity, 0, r, w), T.sts, "sts")

    ts(T.e16[:], T.row[:], T.pf[:, 0:1], ALU.is_equal, r=["row", "pf0"], w=["e16"])
    ts(T.g8[:], T.row[:, 0:8], T.pf[:, 1:2], ALU.is_equal, r=["row", "pf0"], w=["g8"])
    ts(T.ob[:], T.grow[:], T.pf[:, 1:2], ALU.is_equal, r=["grow", "pf0"], w=["ob"])
    ts(T.obn[:], T.grow[:], T.pf[:, 1:2], ALU.is_equal, -1.0, ALU.mult, r=["grow", "pf0"], w=["obn"])
    op("G", lambda: g.affine_select(T.n1[:], T.obn[:], [[-1, 128]], ALU.is_gt, 0.0, 0, 1), ["obn"], ["n1"])
    op("G", lambda: g.affine_select(T.n2[:], T.n1[:], [[-1, 128]], ALU.not_equal, -32768.0, 0, 1), ["n1"], ["n2"])

    def clear():
        op("G", lambda: g.iota(T.win[:, 0:NS], [[0, NS]], 0, 0, **FL), (), ["win"])
        op("G", lambda: g.iota(T.ws[:, 0:NS], [[0, NS]], 0, 0, **FL), (), ["ws"])

    clear()
    for c in range(16):
        op("G", lambda: g.affine_select(blk(T.rmp, c), T.rm[:, 15 - c:2048:16], [[0, 128]],
                                        ALU.is_ge, 0.0, 0, 0), ["rm"], ["rmp"])

    E = T.e16
    for n in ("cb", "ch", "co", "cc"):
        ms(T[n][:], 0.0, [n])
    ts(T.pf[:, 2:3], E[:, 0:1], 16.0, ALU.mult, E[:, 1:2], ALU.add, ["e16"], ["pf2"])
    ts(T.pf[:, 3:4], E[:, 5:6], 16.0, ALU.mult, E[:, 6:7], ALU.add, ["e16"], ["pf3"])
    ts(T.pf[:, 4:5], E[:, 0:1], 592.0, ALU.mult, E[:, 3:4], ALU.add, ["e16"], ["pf4"])
    ms(T.dr[:], 0.0, ["dr"])
    ts(T.pf[:, 5:6], E[:, 1:2], 37.0, ALU.mult, T.pf[:, 4:5], ALU.add, ["e16", "pf4"], ["pf5"])
    ts(T.cb[:, 15:143:16], T.g8[:], T.pf[:, 2:3], ALU.mult, r=["g8", "pf2"], w=["cb"])
    ts(T.pf[:, 6:7], E[:, 2:3], 47.0, ALU.mult, T.pf[:, 5:6], ALU.add, ["e16", "pf5"], ["pf6"])
    ts(T.co[:, 15:143:16], T.g8[:], T.pf[:, 3:4], ALU.mult, r=["g8", "pf3"], w=["co"])
    ts(T.pf[:, 7:8], E[:, 4:5], 64.0, ALU.mult, T.pf[:, 6:7], ALU.add, ["e16", "pf6"], ["pf7"])
    cp("V", T.cc[:, 15:143:16], T.g8[:], ["g8"], ["cc"])
    ts(T.ch[:, 15:143:16], T.g8[:], T.pf[:, 7:8], ALU.mult, r=["g8", "pf7"], w=["ch"])
    ms(T.dr[:, 0:512:8], 1048576.0, ["dr"])
    ms(T.R[:, NS:NS + 16], 0.0, ["Rz"])
    ms(T.two[:], -1.0, ["two"])
    ts(T.dump[:], T.krow[:], 16.0, ALU.mult, T.pf[:, 0:1], ALU.add, ["krow", "pf0"], ["dump"])
    offsets(1, 5)
    ts(T.dump[:], T.dump[:], 4096.0, ALU.add, r=["dump"], w=["dump"])

    def gz(e, z, off, key):
        cp(e, T.Z[:, 512 * z:512 * z + 512], T.nz[:, 0:4096].indirect(off), ["nz", key], ["Z%d" % z])

    def gk(e, z, off, key):
        cp(e, T.K[:, 512 * z:512 * z + 512], T.kd[:, 0:2048].indirect(off), ["kd", key], ["K%d" % z])

    ring = {"p": 0}

    def gp(z, off, key):
        n = ring["p"]
        ring["p"] += 1
        p = n % 4
        tt(T.P[:, 512 * p:512 * p + 512], T.w[:, 0:2048].indirect(off), T.Z[:, 512 * z:512 * z + 512], ALU.mult,
           ["w", key, "Z%d" % z], ["P%d" % p])
        return n

    def part(bank, c, buf, slot, b, st, sp):
        mat = {"Z": "iz", "P": "ip", "K": "ik"}[buf]
        mm(T[bank][:, c:c + 128], T[buf][:, 512 * slot + b:512 * slot + 512:4], T[mat][:], st, sp,
           ["%s%d" % (buf, slot), mat], [bank, bank + "d"])

    def turn(n, z):
        bank = ("TA", "TB")[n % 2]
        for b in range(4):
            part(bank, 128 * b, "Z", z, b, True, False)
            part(bank, 128 * b, "P", n % 4, b, False, False)
            part(bank, 128 * b, "K", z, b, False, True)

    def scan(n, banks=None):
        sb, j = "sb%d" % (n % 2), 4 * (n % 2)
        for b in range(4):
            bank, c = (banks[b], 0) if banks else (("TA", "TB")[n % 2], 128 * b)
            run(T.so[:, :, j + b], T.dk[:], T[bank][:, c:c + 128], ALU.max, [bank + "d", "dk"], [bank, "so%d" % (j + b)])
        cp("V", T[sb][:, 3:35:4, :], T.so[:, 15:128:16, j:j + 4], ["so%d" % (j + b) for b in range(4)], [sb])

    def back(n, bank, c0, key):
        sb = "sb%d" % (n % 2)
        for il in range(4):
            mm(T[bank][:, c0:c0 + 32], T[sb][:, 3 - il:35 - il, :], T.i32[:, il:128:4], il == 0, il == 3,
               [sb, "i32"], [bank, key])

    def draw(nch, ob, oh, kb, kh, c0, key):
        z0, L = 8, nch - 1
        cs = [slice(32 * c, 32 * c + 32) for c in range(nch)]
        gz("S", z0, oh[:, cs[0]], kh)
        gz("V", z0 + 1, oh[:, cs[1]], kh)
        gk("S", z0, ob[:, cs[0]], kb)
        n = [gp(z0, ob[:, cs[0]], kb)]
        turn(n[0], z0)
        n.append(gp(z0 + 1, ob[:, cs[1]], kb))
        for c in range(1, L):
            gz("S", z0 + c + 1, oh[:, cs[c + 1]], kh)
            gk("S", z0 + c, ob[:, cs[c]], kb)
            scan(n[c - 1])
            turn(n[c], z0 + c)
            back(n[c - 1], "PL", c0 + 32 * (c - 1), key)
            n.append(gp(z0 + c + 1, ob[:, cs[c + 1]], kb))
        gk("S", z0 + L, ob[:, cs[L]], kb)
        scan(n[L - 1])
        banks = ("G0", "G1", "R0", "R1")
        for b, bank in enumerate(banks):
            part(bank, 0, "Z", z0 + L, b, True, False)
            part(bank, 0, "P", n[L] % 4, b, False, False)
        for b, bank in enumerate(banks):
            part(bank, 0, "K", z0 + L, b, False, True)
        back(n[L - 1], "PL", c0 + 32 * (L - 1), key)
        scan(n[L], banks)
        back(n[L], "PL", c0 + 32 * L, key)

    fz = {"g": 0, "p": 0, "t": 0, "s": 0, "n": {}}

    def fill_g(k):
        for _ in range(k):
            u = fz["g"]
            fz["g"] += 1
            a = 128 + 32 * u
            gz("S", u % 8, T.oh0[:, a:a + 32], "hoff1")
            gk("S", u % 8, T.ob0[:, a:a + 32], "boff1")

    def fill_p():
        u = fz["p"]
        fz["p"] += 1
        a = 128 + 32 * u
        fz["n"][u] = gp(u % 8, T.ob0[:, a:a + 32], "boff1")

    def fill_t():
        u = fz["t"]
        fz["t"] += 1
        turn(fz["n"][u], u % 8)

    def fill_c(t):
        cp("V", blk(T.V, t), blk(T.PF, t % 2), ["PF%d" % (t % 2)], ["PF", "V%d" % t])

    def fill_s():
        u = fz["s"]
        fz["s"] += 1
        scan(fz["n"][u])
        t = 1 + u // 4
        if u % 8 == 5:
            fill_c(t - 1)
        back(fz["n"][u], "PF", 128 * (t % 2) + 32 * (u % 4), "PF%d" % (t % 2))

    def fill(k):
        for _ in range(k):
            fill_p()
            fill_t()
            if fz["p"] - fz["s"] > 1:
                fill_s()
        while fz["s"] < fz["p"]:
            fill_s()

    peers = [(me + d) % NR for d in range(1, NR)]
    sent = [0]

    def send(kind, r, piece, keys):
        deps("G", keys, [])
        xs = []
        for n, q in enumerate(peers):
            rid, pid, _ = topo.addr(T.cores[q])
            xs.append(RemoteDMATransfer(dst_ids=[DstId(rid=rid, pnc=pid)],
                                        dma_engine_mask=1 << topo.engines(core, T.cores[q])[n],
                                        remote_sem=T.sem["a%s%d" % (kind, r)],
                                        src=piece(T["s%s%d" % (kind, r)], q), dst=piece(T["l%s%d" % (kind, r)], me)))
        g.remote_dma_fused(xs, local_sem=T.sem.loc)
        sent[0] += NR - 1
        wr["l%s%d" % (kind, r)] = ("D", "a%s%d" % (kind, r), NR - 1)

    def lists(b, q):
        return b[:, 2 * KS * q:2 * KS * (q + 1)]

    def cols(b, q):
        return b[:, CAP * q:CAP * q + CAP]

    def fld(b, f):
        return b[:, f:2 * KS * NR:2]

    def gather_list(out, cm, rhs, rkeys, bank, key, st=True, sp=True):
        for i in range(16):
            mm(out, T[cm][:, 15 - i:143 - i], rhs(i), st and i == 0, sp and i == 15, [cm] + rkeys, [bank, key])

    def settle(r0):
        tt(T.e[:], blk(T.PL, 3), T.e[:], ALU.mult, ["keep", "e"], ["PL", "e"])
        if r0 == 0:
            ts(T.one[:], T.e[:], -1.0, ALU.add, r=["e"], w=["one"])
        else:
            f = blk(T.PL, 2)
            tt(f, T.e[:], T.none[:], ALU.mult, ["e", "none"], ["PL", "PLc"])
            tt(T.two[:], T.two[:], T.e[:], ALU.add, ["two", "e"], ["two"])
            tt(T.one[:], f, T.one[:], ALU.add, ["PLc", "one"], ["PL", "one"])
            tt(T.two[:], T.two[:], f, ALU.subtract, ["PLc", "two"], ["PL", "two"])
        if r0 < RO - 1:
            ts(T.none[:], T.one[:], 0.0, ALU.is_lt, r=["one"], w=["none"])

    def device():
        tt(T.e[:], blk(T.PL, 0), T.base[:], ALU.add, ["PLv", "base"], ["PL", "e"])

    draw(4, T.ob0, T.oh0, "boff0", "hoff0", 0, "PLv")
    cp("V", T.si[:], blk(T.PL, 0), ["PLv"], ["PL", "si"])

    for r in range(RO):
        last = r == RO - 1
        sq, lq, sn, ln, sr, lr = (T["%s%d" % (n, r)] for n in ("sq", "lq", "sn", "ln", "sr", "lr"))
        kq, kn, kr = "lq%d" % r, "ln%d" % r, "lr%d" % r
        ts(ti[0], T.si[:], 127, AND, r=["si"], w=["ti0"])
        ts(ti[1], T.si[:], 7, SHR, 15, AND, ["si"], ["ti1"])
        ts(blk(T.fl, 0), ti[0], 1.0, ALU.mult, r=["ti0"], w=["fl0"])
        ts(blk(T.fl, 1), ti[1], -1.0, ALU.mult, 15.0, ALU.add, ["ti1"], ["fl1"])
        ts(T.ccl[:], T.si[:], 7, SHR, 65543, AND, ["si"], ["ccl"])
        fields = [(0, 0, "fl0"), (1, 1, "fl1")]
        if r > 0:
            fields = [(2, 2, "fl2")] + fields
        spread(1, T.fl, fields)
        if not last:
            fill_g(3)
        ts(T.ccb[:], T.ccl[:], 1.0, ALU.mult, r=["ccl"], w=["ccb"])
        pu, pa = blk(T.PF, 2), blk(T.PF, 3)
        ts(pu, T.ccl[:], -float(CAP), ALU.mult, 32767.0 + 7 * CAP, ALU.add, ["ccl"], ["PF", "PF2"])
        for q in range(NR):
            ts(T.m[:, q:1024:8], T.ccb[:], float(7 - q), ALU.is_equal, r=["ccb"], w=["m%d" % q])
        for q in range(NR):
            run(T.sc[:, q:1024:8], T.m[:, q:1024:8], T.m[:, q:1024:8], ALU.max, ["m%d" % q], ["sc%d" % q])
        for h in range(2):
            bank = "R%d" % h
            mm(T[bank][:], T.n2[:], T.m[:, 512 * h:512 * h + 512], True, False,
               ["n2"] + ["m%d" % q for q in range(NR)], [bank, bank + "d"])
            mm(T[bank][:], T.ob[:], T.sc[:, 512 * h:512 * h + 512], False, True,
               ["ob"] + ["sc%d" % q for q in range(NR)], [bank, bank + "d"])
        rows(lambda o, p, i, rr, w: tt(o, p, T.sts[:, i:1024:16], ALU.add, rr + ["sts"], w), T.ps, "ps")
        spread(0, T.fl, fields)
        for h in range(2):
            bank = "R%d" % h
            run(T.qs[:, 512 * h:512 * h + 512], T.dr[:], T[bank][:], ALU.min, [bank + "d", "dr"], [bank, "qs%d" % h])
        qv = T.qs[:, 7:1024:8]
        ts(pa, qv, 32767.0 - (CAP - 1), ALU.add, 8192.0, ALU.mult, ["qs0", "qs1"], ["PF", "PF3"])
        tt(pu, pu, qv, ALU.add, ["qs0", "qs1", "PF2"], ["PF", "PF2"])
        tt(tf[0], pa, T.dump[:], ALU.min, ["PF3", "dump"], ["PF", "tf0"])
        tt(tf[1], pu, tf[0], ALU.max, ["PF2", "tf0"], ["PF", "tf1"])
        cp("V", T.pos[:], tf[1], ["tf1"], ["pos"])
        op("S", lambda: S.activation(T.ws[:, 0:6144].indirect(T.pos[:, 64:128]), T.ps[:], ACT.Silu), ["pos", "ps"], ["ws"])
        act(T.wb[:], T.ws[:, 0:NS], ACT.Relu, 1, ["ws"], ["wb"])
        rows(lambda o, p, i, rr, w: cp("V", o, p, rr, w), T.pay, "pay")
        tt(T.win[:, 0:6144].indirect(T.pos[:, 0:64]), T.pay[:], T.st[:], ALU.add, ["pos", "pay", "st"], ["win"])
        if not last:
            fill_g(1)
        for grp in ((("R0", "ch"), ("R1", "cb")), (("G0", "co"),)):
            for buf in ("win", "wb"):
                for bank, cm in grp:
                    gather_list(T[bank][:, 0:96], cm, lambda i: T[buf][:, i:NS:16], [buf], bank, bank + "d",
                                buf == "win", buf == "wb")
        ts(T.pos2[:], tf[1], float(NS), ALU.min, r=["tf1"], w=["pos2"])
        if r > 0:
            device()
            settle(r - 1)
        ts(T.base[:], T.ccl[:], -2048.0, ALU.mult, 7 * 2048.0 - 2047.0, ALU.add, ["ccl"], ["base"])
        if not last:
            fill_p()
            ts(T.go[:], tf[1], float(NS), ALU.is_lt, r=["tf1"], w=["go"])
        cp("V", T.rhi[:], T.R0[:, 0:96], ["R0d"], ["R0", "rhi"])
        ts(fld(sq, 1), T.rhi[:], 4095, AND, r=["rhi"], w=["sq1"])
        cp("V", fld(sq, 0), T.R1[:, 0:96], ["R1d"], ["R1", "sq0"])
        send("q", r, lists, ["sq0", "sq1"])
        cp("V", lists(lq, me), lists(sq, me), ["sq0", "sq1"], [kq + "o"])
        if r > 0:
            tt(T.cv[:], T.one[:], T.base[:], ALU.subtract, ["one", "base"], ["cv"])
        if not last:
            fill_p()
        cp("V", T.oo[:], T.G0[:, 0:96], ["G0d"], ["G0", "oo"])
        cp("S", sn[:], T.nd[:, 0:2048].indirect(T.oo[:]), ["nd", "oo"], ["sn"])
        send("n", r, cols, ["sn"])
        cp("S", cols(ln, me), cols(sn, me), ["sn"], [kn + "o"])
        if r > 0:
            ts(T.cv[:], T.cv[:], 1.0, ALU.add, r=["cv"], w=["cv"])
        if not last:
            clear()
            fill_t()
            fill_t()
            fill_s()
            fill(AHEAD - 2)
        cp("V", T.rh2[:], fld(lq, 1), [kq, kq + "o"], ["rh"])
        cp("V", T.rb2[:], fld(lq, 0), [kq, kq + "o"], ["rb"])
        draw(3, T.rb2, T.rh2, "rb", "rh", 128, "PLo")
        if not last:
            fill_g(4)
        cp("V", T.oi[:], T.PL[:, 128:224], ["PLo"], ["PL", "oi"])
        ts(T.ox[:], T.oi[:], 2047, AND, r=["oi"], w=["ox"])
        cp("V", T.oxu[:], T.ox[:], ["ox"], ["oxu"])
        for h in range(2):
            tt(T.cmp[:, 768 * h:768 * h + 768], T.rmp[:, 0:2048].indirect(T.oxu[:, 48 * h:48 * h + 48]),
               ln[:, 768 * h:768 * h + 768], ALU.is_ge, ["rmp", "oxu", kn, kn + "o"], ["cmp%d" % h])
            gather_list(T.PL[:, 256 + 48 * h:304 + 48 * h], "cc",
                        lambda i: T.cmp[:, 768 * h + i:768 * h + 768:16], ["cmp%d" % h], "PL", "PLc")
        ts(T.oc[:], T.oi[:], 7, SHR, 15, AND, ["oi"], ["oc"])
        ts(T.ok[:], T.oi[:], 127, AND, r=["oi"], w=["ok"])
        ts(fld(sr, 1), T.oc[:], -1.0, ALU.mult, 15.0, ALU.add, ["oc"], ["sr1"])
        ts(T.PL[:, 128:224], T.PL[:, 256:352], 15.5, ALU.is_ge, 128.0, ALU.mult, ["PLc"], ["PL", "PLo"])
        tt(fld(sr, 0), T.PL[:, 128:224], T.ok[:], ALU.add, ["PLo", "ok"], ["PL", "sr0"])
        send("r", r, lists, ["sr0", "sr1"])
        cp("V", lists(lr, me), lists(sr, me), ["sr0", "sr1"], [kr + "o"])
        if not last:
            fill(8 - AHEAD)
            if r == 0:
                ts(T.tb[:], T.go[:], 2.0, ALU.mult, r=["go"], w=["tb"])
                A, ka, fix, kf = blk(T.V, 1), ["V1"], blk(T.PF, 0), "PF0"
                tt(fix, fix, T.si[:], ALU.subtract, [kf, "si"], ["PF", kf])
                tt(blk(T.V, 2), fix, T.si[:], ALU.add, [kf, "si"], ["PF", "V2"])
            else:
                ts(tf[4], T.none[:], -8388608.0, ALU.mult, 8388608.0, ALU.add, ["none"], ["tf4"])
                ts(tf[5], T.go[:], 2.0, ALU.mult, r=["go"], w=["tf5"])
                tt(T.tb[:], tf[5], T.t[:], ALU.add, ["tf5", "t"], ["tb"])
                fill_c(4)
                for t in (1, 2, 0):
                    ts(blk(T.PF, t), T.t[:], float(t), ALU.is_equal, r=["t"], w=["PF", "PF%d" % t])
                for t in range(3):
                    for j in range(2):
                        tt(tf[2 * (t % 2) + j] if t else blk(T.AB, j), blk(T.PF, t), blk(T.V, t + 1 + j),
                           ALU.mult, ["PF%d" % t, "V%d" % (t + 1 + j)],
                           ["PF", ("tf%d" % (2 * (t % 2) + j)) if t else "AB%d" % j])
                tt(blk(T.PF, 0, 2), blk(T.tf, 2, 2), T.AB[:], ALU.add, ["tf2", "tf3", "AB0", "AB1"], ["PF", "PF0", "PF1"])
                tt(blk(T.PF, 0, 2), blk(T.PF, 0, 2), blk(T.tf, 0, 2), ALU.add, ["PF0", "tf0", "tf1"], ["PF", "PF0", "PF1"])
                tt(blk(T.AB, 0), blk(T.PF, 0), tf[4], ALU.add, ["PF0", "tf4"], ["PF", "AB0"])
                A, ka, fix, kf = blk(T.AB, 0), ["AB0"], blk(T.PF, 1), "PF1"
                tt(fix, fix, T.si[:], ALU.subtract, [kf, "si"], ["PF", kf])
            tt(blk(T.PF, 2), fix, T.go[:], ALU.mult, [kf, "go"], ["PF", "PF2"])
            tt(T.B[:], blk(T.PF, 2), T.si[:], ALU.add, ["PF2", "si"], ["PF", "B"])
            tt(T.D[:], A, T.B[:], ALU.subtract, ka + ["B"], ["D"])
        for b, bank in enumerate(("G0", "R0", "G1", "R1")):
            for i in range(4 * b, 4 * b + 4):
                for f in range(2):
                    mm(T[bank][:, 96 * (i % 4):96 * (i % 4) + 96], T.am[:, i, 7 - f:135 - f], fld(lr, f),
                       f == 0, f == 1, ["am", kr, kr + "o"], [bank, bank + "d"])
            for i in range(4 * b, 4 * b + 4):
                cp("V" if last and b % 2 else "S", T.R[:, i:NS:16], T[bank][:, 96 * (i % 4):96 * (i % 4) + 96],
                   [bank + "d"], [bank, "R%dx" % b])
        rk = ["R0x", "R1x", "R2x", "R3x", "Rz", "pos2"]
        for h in range(2):
            for j, e in enumerate(("S", "V")):
                c = 2 * h + j
                cp(e, T.Rg[:, 512 * c:512 * c + 512], T.R[:, 0:NS + 16].indirect(T.pos2[:, 32 * c:32 * c + 32]), rk,
                   ["Rg%d" % c])
            gather_list(T.PL[:, 64 * h:64 * h + 64], "cb", lambda i: T.Rg[:, 1024 * h + i:1024 * h + 1024:16],
                        ["Rg%d" % (2 * h), "Rg%d" % (2 * h + 1)], "PL", "PLv")
        v, keep, tmp = blk(T.PL, 0), blk(T.PL, 3), blk(T.PL, 1)
        ts(keep, v, 2048.0, ALU.is_ge, r=["PLv"], w=["PL", "keep"])
        if r > 0:
            tt(T.ne[:], v, T.cv[:], ALU.not_equal, ["PLv", "cv"], ["PL", "ne"])
            if last:
                device()
            tt(keep, keep, T.ne[:], ALU.mult, ["keep", "ne"], ["PL", "keep"])
        if not last:
            tt(T.t[:], T.tb[:], keep, ALU.subtract, ["keep", "tb"], ["PL", "t"])
            tt(tmp, keep, T.D[:], ALU.mult, ["keep", "D"], ["PL", "PLo"])
            ts(blk(T.fl, 2), T.t[:], 13.0, ALU.mult, r=["t"], w=["fl2"])
            tt(T.si[:], tmp, T.B[:], ALU.add, ["PLo", "B"], ["PL", "si"])

    settle(RO - 1)
    deps("Y", ["one"], [])
    g.sync.dma_start(T.ya[:], T.one[:]).then_inc(T.sem.oa, 16)
    deps("S", ["two"], [])
    g.scalar.dma_start(T.yb[:], T.two[:]).then_inc(T.sem.obs, 16)
    for e in ("V", "S", "P", "G"):
        g.wait_ge(T.sem["c" + e], cnt[e])
    g.wait_ge(T.sem.loc, sent[0])
    g.wait_ge(T.sem.oa, 16)
    g.wait_ge(T.sem.obs, 16)
